import numpy as np
import ml_dtypes


def mxq(x, axis, fmt="e4m3"):
    dtype, down = {"e4m3": (ml_dtypes.float8_e4m3fn, 7), "e5m2": (ml_dtypes.float8_e5m2, 14)}[fmt]
    v = np.moveaxis(np.asarray(x, np.float32).astype(ml_dtypes.bfloat16).astype(np.float64), axis, -1)
    blocks = v.reshape(v.shape[:-1] + (-1, 32))
    amax = np.abs(blocks).max(-1, keepdims=True)
    byte = np.maximum(np.where(amax > 0, np.frexp(amax)[1] - 1 + 127, 0) - down, 1)
    scale = np.exp2(byte - 127.0)
    codes = (blocks / scale).astype(np.float32).astype(dtype).astype(np.float64)
    return np.moveaxis((codes * scale).reshape(v.shape), -1, axis)


WIDE = False


def mx_kscale(k):
    if not WIDE:
        return np.ones(k)
    levels = np.array([10, -10, 5, -5, 0])
    if k % 512:
        return np.exp2(np.random.permutation(np.resize(levels, k // 32))).repeat(32)
    a = np.empty((k // 512, 16))
    for p in range(k // 512):
        a[p, :8] = np.random.permutation(np.resize(levels, 8))
        for g in range(8):
            far = levels[np.abs(levels - a[p, g]) >= 10]
            a[p, g + 8] = far[np.random.randint(len(far))]
    return np.exp2(a.ravel()).repeat(32)


def f64(x):
    return np.asarray(x).astype(np.float64)


def striped(idx):
    return np.tile(idx.reshape(-1, 16).T, (8, 1)).astype(np.uint16)


def unstriped(offs):
    return offs[:16].T.reshape(-1).astype(np.int64)


def striped8(idx):
    return np.concatenate([x.reshape(-1, 16).T for x in idx]).astype(np.uint16)


def runs(offs, k):
    lists = np.stack([offs[16 * r : 16 * r + 16].T.reshape(-1) for r in range(8)]).astype(np.int64)
    return lists[np.arange(k) % 512 // 64]


def pack_weight(w):
    k, n = w.shape
    w = f64(np.asarray(w, np.float32).astype(ml_dtypes.bfloat16)).reshape(k // 32, 32, n)
    amax = np.abs(w).max(1)
    byte = np.clip(np.where(amax > 0, np.frexp(amax)[1] - 1 + 127 - 7, 1), 1, 254)
    scaled = (w * np.exp2(127.0 - byte)[:, None, :]).reshape(k, n).astype(np.float32)
    words = np.ascontiguousarray(scaled.reshape(k // 512, 128, 4, n).transpose(0, 1, 3, 2)).astype(ml_dtypes.float8_e4m3fn).view(np.uint8)
    return words, np.ascontiguousarray(byte.astype(np.uint8).reshape(k // 512, 16, n))


def unpack_weight(words, scales):
    g, p, n, _ = words.shape
    vals = np.ascontiguousarray(words).view(ml_dtypes.float8_e4m3fn).astype(np.float64) * np.repeat(np.exp2(scales.astype(np.float64) - 127.0), 8, axis=1)[..., None]
    return vals.transpose(0, 1, 3, 2).reshape(g * 512, n)


def sigmoid(v):
    return 1.0 / (1.0 + np.exp(-np.maximum(v, -700.0)))

def planes(y):
    n, m = y.shape
    v = y.astype(np.float32).astype(ml_dtypes.bfloat16).astype(np.float64).reshape(n // 32, 32, m)
    top = np.abs(v).max(1)
    byte = np.clip(np.where(top > 0, np.frexp(top)[1] - 1 + 127 - 7, 1), 1, 254)
    codes = (v * np.exp2(127.0 - byte)[:, None, :]).reshape(n, m).astype(np.float32).astype(ml_dtypes.float8_e4m3fn).view(np.uint8)
    words = codes.reshape(n // 512, 128, 4, m).transpose(0, 1, 3, 2)
    return np.ascontiguousarray(words), np.ascontiguousarray(byte.astype(np.uint8).reshape(n // 512, 16, m))


K, T, S, G, H, W, C, U = 512, 1024, 256, 2048, 512, 128, 512, 1024


def setup_inputs():
    n = np.random.standard_normal
    s = mx_kscale(K)[:, None]
    packed_xT = pack_weight(n((K, T)) * s)
    packed_dT = pack_weight(n((K, G)) / s)
    perm = np.random.permutation(S)
    return {
        "x_words": packed_xT[0],
        "x_scales": packed_xT[1],
        "d_words": packed_dT[0],
        "d_scales": packed_dT[1],
        "gs": (np.random.uniform(0.5, 1.5, (K, 1)) / s).astype(np.float32),
        "offs": striped(np.random.permutation(T)[:S]),
        "k1": striped8(np.random.randint(0, G, (8, H))),
        "n1": striped(perm[:W]),
        "n2": striped(perm[W:]),
        "cand": striped(np.random.permutation(T)[:C]),
        "n3": striped(np.random.randint(0, S, U)),
    }


def reference(x_words, x_scales, d_words, d_scales, gs, offs, k1, n1, n2, cand, n3):
    x_cand = unpack_weight(x_words, x_scales)[:, unstriped(cand)]
    d_k1 = unpack_weight(d_words, d_scales)[np.arange(K)[:, None], runs(k1, K)]
    xq = unpack_weight(x_words, x_scales)[:, unstriped(offs)]
    h = 0.0625 * (d_k1.T @ xq)
    pb = h[:, unstriped(n2)]
    pa = h[:, unstriped(n1)]
    rb = pb * sigmoid(pb - pa)
    ra = pa * sigmoid(pa - pb)
    ds = np.zeros((H, S))
    ds[:, unstriped(n1)] = ra
    dt = ds.copy()
    dt[:, unstriped(n2)] = rb
    z = f64(gs) * dt
    s = 0.0625 * ((x_cand.T @ mxq(z, 0, "e4m3")))
    mb = s[:, unstriped(n3)]
    mn = mb.reshape(C, S, 4).min(axis=2)
    mx = mb.reshape(C, S, 4).max(axis=2)
    out_0 = np.maximum(s, mn) - (0.5 * mx)
    return (out_0,) + planes(out_0)

@@ -1,0 +1,240 @@
+from contextlib import ExitStack
+
+import concourse.mybir as mybir
+
+F32 = mybir.dt.float32
+BF16 = mybir.dt.bfloat16
+I32 = mybir.dt.int32
+U32 = mybir.dt.uint32
+U16 = mybir.dt.uint16
+U8 = mybir.dt.uint8
+FP8X4 = mybir.dt.float8_e4m3fn_x4
+ALU = mybir.AluOpType
+ACT = mybir.ActivationFunctionType
+
+K, T, S, G, H, W, C, U = 512, 1024, 256, 2048, 512, 128, 512, 1024
+P = 128
+PACK = 4
+FLOPS = 2 * K * H * S + 2 * H * C * S
+HALF = U // 2
+WIN = HALF + 16
+
+
+def tile_picked_pqcduelgmid_none_po_kernel(tc, x_words, x_scales, d_words, d_scales, gs, offs, k1, n1, n2, cand, n3, out_0, out_1, out_2):
+    nc = tc.nc
+    with ExitStack() as ctx:
+        keep = ctx.enter_context(tc.tile_pool(name="keep", bufs=1))
+        psum = ctx.enter_context(tc.psum_pool(name="psum", bufs=1))
+
+        def sb(name, shape, dtype):
+            return keep.tile(shape, dtype, name=name, align_bytes=64)
+
+        def load_list(name, src):
+            t = keep.tile(list(src.shape), U16, name=name)
+            nc.sync.dma_start(t[:], src)
+            return t
+
+        k1_t = load_list("k1_t", k1)
+        d_scale_tab = sb("d_scale_tab", [P, G], U8)
+        nc.scalar.dma_start(d_scale_tab[:].bitcast(I32), d_scales[0].bitcast(I32).unsqueeze(1).broadcast_to([16, 8, G // 4]))
+        offs_t = load_list("offs_t", offs)
+        x_scale_tab = sb("x_scale_tab", [P, T], U8)
+        nc.scalar.dma_start(
+            x_scale_tab[:].bitcast(I32),
+            x_scales[0].bitcast(I32).unsqueeze(1).broadcast_to([16, 8, T // 4]),
+        )
+        n1_t = load_list("n1_t", n1)
+        n2_t = load_list("n2_t", n2)
+        d_tab = sb("d_tab", [P, G], I32)
+        nc.sync.dma_start(d_tab[:], d_words[0].rearrange("p n t -> p (n t)").bitcast(I32))
+        x_tab = sb("x_tab", [P, T], I32)
+        nc.sync.dma_start(x_tab[:], x_words[0].rearrange("p n t -> p (n t)").bitcast(I32))
+        cand_t = load_list("cand_t", cand)
+        n3_t = load_list("n3_t", n3)
+        gs_t = sb("gs_t", [P, PACK], F32)
+        nc.gpsimd.dma_start(gs_t[:], gs.rearrange("(p t) o -> p (t o)", t=PACK))
+
+        plane1 = sb("plane1", [P, H + S], U8)
+        nc.vector.memset(plane1[:].bitcast(I32), 0)
+        xc_plane = sb("xc_plane", [P, C], U8)
+        nc.vector.memset(xc_plane[:].bitcast(I32), 0)
+
+        def place_rows(plane, rows, engines):
+            for a in range(4):
+                engines[a % len(engines)].dma_start(plane[a:P:32, :].bitcast(I32), rows[8 * a : P : 32, :].bitcast(I32))
+
+        s_win = [sb("s_win%d" % t, [P, WIN], F32) for t in range(PACK)]
+        for t in range(PACK):
+            nc.vector.memset(s_win[t][:, S:WIN], 0.0)
+
+        d_bytes = sb("d_bytes", [P, H], U8)
+        nc.vector.tensor_copy(d_bytes[:], d_scale_tab[:].indirect(k1_t[:]))
+        xq_bytes = sb("xq_bytes", [P, S], U8)
+        nc.vector.tensor_copy(xq_bytes[:], x_scale_tab[:].indirect(offs_t[:]))
+        rows1 = sb("rows1", [P, H + S], U8)
+        nc.vector.tensor_copy(rows1[:, 0:H].rearrange("p (t m) -> p m t", t=PACK), d_bytes[:].rearrange("p (m t) -> p m t", t=PACK))
+        nc.vector.tensor_copy(rows1[:, H : H + S].bitcast(I32), xq_bytes[:].bitcast(I32))
+        place_rows(plane1, rows1, [nc.scalar, nc.sync])
+        d_picked = sb("d_picked", [P, H], U32)
+        nc.vector.tensor_copy(d_picked[:], d_tab[:].bitcast(U32).indirect(k1_t[:]))
+        d_dealt = sb("d_dealt", [P, H], U32)
+        nc.vector.tensor_copy(d_dealt[:].rearrange("p (t m) -> p m t", t=PACK), d_picked[:].rearrange("p (m t) -> p m t", t=PACK))
+        xq_words = sb("xq_words", [P, S], U32)
+        nc.vector.tensor_copy(xq_words[:], x_tab[:].bitcast(U32).indirect(offs_t[:]))
+
+        h_win = []
+        for t in range(PACK):
+            acc = psum.tile([P, S], F32, name="h_acc%d" % t)
+            cols = slice(P * t, P * t + P)
+            nc.tensor.matmul_mx(acc[:], lhsT=d_dealt[:, cols].bitcast(FP8X4), lhsT_scale=plane1[:, cols],
+                                rhs=xq_words[:].bitcast(FP8X4), rhs_scale=plane1[:, H : H + S], start=True, stop=True)
+            win = sb("h_win%d" % t, [P, S], F32)
+            nc.vector.tensor_scalar(win[:], acc[:], 0.0625 * 0.5, None, ALU.mult)
+            h_win.append(win)
+
+        pa = [sb("pa%d" % g, [P, 2, W], F32) for g in range(2)]
+        npb = [sb("npb%d" % g, [P, 2, W], F32) for g in range(2)]
+        diff = [sb("diff%d" % g, [P, 2, W], F32) for g in range(2)]
+        th = [sb("th%d" % g, [P, 2, W], F32) for g in range(2)]
+        ra = [sb("ra%d" % g, [P, 2, W], F32) for g in range(2)]
+        rb = [sb("rb%d" % g, [P, 2, W], F32) for g in range(2)]
+        dt = [sb("dt%d" % t, [P, S], F32) for t in range(PACK)]
+        z_bf = sb("z_bf", [P, S, PACK], BF16)
+        xc_words = sb("xc_words", [P, C], U32)
+        xc_scales = sb("xc_scales", [P, C], U8)
+
+        def fetch(t):
+            g, u = divmod(t, 2)
+            nc.scalar.activation(pa[g][:, u, :], h_win[t][:].indirect(n1_t[:]), ACT.Copy)
+            nc.scalar.activation(npb[g][:, u, :], h_win[t][:].indirect(n2_t[:]), ACT.Copy, scale=-1.0)
+
+        def duel_diff(g):
+            nc.vector.tensor_tensor(diff[g][:], pa[g][:], npb[g][:], ALU.add)
+
+        def duel_tanh(g):
+            nc.scalar.activation(th[g][:], diff[g][:], ACT.Tanh)
+
+        def duel_weigh(g):
+            nc.vector.scalar_tensor_tensor(ra[g][:], th[g][:], 1.0, pa[g][:], ALU.add, ALU.mult)
+            nc.vector.scalar_tensor_tensor(rb[g][:], th[g][:], 1.0, npb[g][:], ALU.subtract, ALU.mult)
+
+        def put(src, lst, t):
+            g, u = divmod(t, 2)
+            nc.scalar.activation(dt[t][:].indirect(lst[:]), src[g][:, u, :], ACT.Copy)
+
+        def weigh_round(t):
+            nc.vector.tensor_scalar(z_bf[:, :, t], dt[t][:], gs_t[:, t : t + 1], None, ALU.mult)
+
+        def pick_cand(i):
+            lst = cand_t[:, 16 * i : 16 * i + 16]
+            ms = slice(64 * i, 64 * i + 64)
+            nc.vector.tensor_copy(xc_words[:].rearrange("p (t m) -> p m t", t=PACK)[:, ms, :], x_tab[:].bitcast(U32).indirect(lst))
+            nc.vector.tensor_copy(xc_scales[:].rearrange("p (t m) -> p m t", t=PACK)[:, ms, :], x_scale_tab[:].indirect(lst))
+
+        fetch(0)
+        fetch(1)
+        duel_diff(0)
+        fetch(2)
+        duel_tanh(0)
+        duel_weigh(0)
+        fetch(3)
+        duel_diff(1)
+        put(ra, n1_t, 0)
+        put(ra, n1_t, 1)
+        duel_tanh(1)
+        duel_weigh(1)
+        pick_cand(0)
+        pick_cand(1)
+        place_rows(xc_plane, xc_scales, [nc.sync])
+        put(rb, n2_t, 0)
+        put(rb, n2_t, 1)
+        weigh_round(0)
+        weigh_round(1)
+        put(ra, n1_t, 2)
+        put(ra, n1_t, 3)
+        put(rb, n2_t, 2)
+        weigh_round(2)
+        put(rb, n2_t, 3)
+        weigh_round(3)
+
+        z_words = sb("z_words", [P, S], U32)
+        z_scales = sb("z_scales", [P, S], U8)
+        nc.vector.quantize_mx(z_words[:].bitcast(FP8X4), z_scales[:], z_bf[:].rearrange("p j t -> p (j t)"))
+
+        for t in range(PACK):
+            acc = psum.tile([P, S], F32, name="s_acc%d" % t)
+            cols = slice(P * t, P * t + P)
+            nc.tensor.matmul_mx(acc[:], lhsT=xc_words[:, cols].bitcast(FP8X4), lhsT_scale=xc_plane[:, cols],
+                                rhs=z_words[:].bitcast(FP8X4), rhs_scale=z_scales[:], start=True, stop=True)
+            if t == 0:
+                nc.scalar.activation(s_win[t][:, 0:S], acc[:], ACT.Copy, scale=0.0625)
+            else:
+                nc.vector.tensor_scalar(s_win[t][:, 0:S], acc[:], 0.0625, None, ALU.mult)
+
+        mb = [sb("mb%d" % t, [P, S, 4], F32) for t in range(PACK)]
+        lo2 = [sb("lo2_%d" % t, [P, 2, S], F32) for t in range(PACK)]
+        hi2 = [sb("hi2_%d" % t, [P, 2, S], F32) for t in range(PACK)]
+        lo = [sb("lo%d" % t, [P, S], F32) for t in range(PACK)]
+        hi = [sb("hi%d" % t, [P, S], F32) for t in range(PACK)]
+        top = [sb("top%d" % t, [P, S], F32) for t in range(PACK)]
+        y = sb("y", [P, PACK, S], F32)
+        y_bf = sb("y_bf", [P, S, PACK], BF16)
+        y_words = sb("y_words", [P, S], U32)
+        y_scales = sb("y_scales", [P, S], U8)
+        out_rows = out_0.rearrange("(p t) j -> p t j", t=PACK)
+        out_words = out_1[0].rearrange("p n t -> p (n t)").bitcast(I32)
+        J = S // 2
+        first, second, whole = slice(0, J), slice(J, S), slice(0, S)
+
+        def members(t, c):
+            nc.scalar.activation(mb[t][:, c, :].rearrange("p j e -> p (j e)"), s_win[t][:].indirect(n3_t[:, c.start // 4 : c.stop // 4]), ACT.Copy)
+
+        def pair(dst, t, c, op):
+            nc.vector.tensor_tensor(dst[t][:, :, c].rearrange("p e j -> p j e"), mb[t][:, c, 0:2], mb[t][:, c, 2:4], op)
+
+        def quad(dst, src, t, c, op):
+            nc.vector.tensor_tensor(dst[t][:, c], src[t][:, 0, c], src[t][:, 1, c], op)
+
+        def larger(t, c):
+            nc.vector.tensor_tensor(top[t][:, c], lo[t][:, c], s_win[t][:, c], ALU.max)
+
+        def result(t, c):
+            nc.vector.scalar_tensor_tensor(y[:, t, c], hi[t][:, c], -0.5, top[t][:, c], ALU.mult, ALU.add)
+            nc.sync.dma_start(out_rows[:, t, c], y[:, t, c])
+
+        def planes(c, cast):
+            cast(y_bf[:, c, :], y[:, :, c].rearrange("p t j -> p j t"))
+            nc.vector.quantize_mx(y_words[:, c].bitcast(FP8X4), y_scales[:, c], y_bf[:, c, :].rearrange("p j t -> p (j t)"))
+            nc.scalar.dma_start(out_words[:, c], y_words[:, c].bitcast(I32))
+
+        last = PACK - 1
+        for t in range(PACK):
+            members(t, first)
+            pair(lo2, t, first, ALU.min)
+            if t:
+                quad(lo, lo2, t - 1, whole, ALU.min)
+            pair(hi2, t, first, ALU.max)
+            if t:
+                quad(hi, hi2, t - 1, whole, ALU.max)
+                larger(t - 1, whole)
+            members(t, second)
+            if t == last:
+                quad(lo, lo2, t, first, ALU.min)
+                result(t - 1, whole)
+                quad(hi, hi2, t, first, ALU.max)
+                larger(t, first)
+            pair(lo2, t, second, ALU.min)
+            if 0 < t < last:
+                result(t - 1, whole)
+            if t == last:
+                result(t, first)
+            pair(hi2, t, second, ALU.max)
+        quad(lo, lo2, last, second, ALU.min)
+        quad(hi, hi2, last, second, ALU.max)
+        larger(last, second)
+        planes(first, nc.scalar.copy)
+        result(last, second)
+        planes(second, nc.vector.tensor_copy)
+        for q in range(4):
+            eng = nc.scalar if q % 2 else nc.sync
+            eng.dma_start(out_2[0, 4 * q : 4 * q + 4, :].bitcast(I32), y_scales[32 * q : 32 * q + 4, :].bitcast(I32))

@@ -26,23 +26,23 @@ def tile_picked_pqcduelgmid_none_po_kernel(tc, x_words, x_scales, d_words, d_sca
         keep = ctx.enter_context(tc.tile_pool(name="keep", bufs=1))
         psum = ctx.enter_context(tc.psum_pool(name="psum", bufs=1))
 
-        def sb(name, shape, dtype):
-            return keep.tile(shape, dtype, name=name, align_bytes=64)
+        def sb(name, shape, dtype, tag=None):
+            return keep.tile(shape, dtype, name=name, tag=tag or name, align_bytes=64)
 
         def load_list(name, src):
             t = keep.tile(list(src.shape), U16, name=name)
             nc.sync.dma_start(t[:], src)
             return t
 
-        k1_t = load_list("k1_t", k1)
-        d_scale_tab = sb("d_scale_tab", [P, G], U8)
-        nc.scalar.dma_start(d_scale_tab[:].bitcast(I32), d_scales[0].bitcast(I32).unsqueeze(1).broadcast_to([16, 8, G // 4]))
         offs_t = load_list("offs_t", offs)
         x_scale_tab = sb("x_scale_tab", [P, T], U8)
         nc.scalar.dma_start(
             x_scale_tab[:].bitcast(I32),
             x_scales[0].bitcast(I32).unsqueeze(1).broadcast_to([16, 8, T // 4]),
         )
+        k1_t = load_list("k1_t", k1)
+        d_scale_tab = sb("d_scale_tab", [P, G], U8)
+        nc.scalar.dma_start(d_scale_tab[:].bitcast(I32), d_scales[0].bitcast(I32).unsqueeze(1).broadcast_to([16, 8, G // 4]))
         n1_t = load_list("n1_t", n1)
         n2_t = load_list("n2_t", n2)
         d_tab = sb("d_tab", [P, G], I32)
@@ -52,7 +52,7 @@ def tile_picked_pqcduelgmid_none_po_kernel(tc, x_words, x_scales, d_words, d_sca
         cand_t = load_list("cand_t", cand)
         n3_t = load_list("n3_t", n3)
         gs_t = sb("gs_t", [P, PACK], F32)
-        nc.gpsimd.dma_start(gs_t[:], gs.rearrange("(p t) o -> p (t o)", t=PACK))
+        nc.sync.dma_start(gs_t[:], gs.rearrange("(p t) o -> p (t o)", t=PACK))
 
         plane1 = sb("plane1", [P, H + S], U8)
         nc.vector.memset(plane1[:].bitcast(I32), 0)
@@ -67,13 +67,13 @@ def tile_picked_pqcduelgmid_none_po_kernel(tc, x_words, x_scales, d_words, d_sca
         for t in range(PACK):
             nc.vector.memset(s_win[t][:, S:WIN], 0.0)
 
-        d_bytes = sb("d_bytes", [P, H], U8)
-        nc.vector.tensor_copy(d_bytes[:], d_scale_tab[:].indirect(k1_t[:]))
         xq_bytes = sb("xq_bytes", [P, S], U8)
         nc.vector.tensor_copy(xq_bytes[:], x_scale_tab[:].indirect(offs_t[:]))
+        d_bytes = sb("d_bytes", [P, H], U8)
+        nc.vector.tensor_copy(d_bytes[:], d_scale_tab[:].indirect(k1_t[:]))
         rows1 = sb("rows1", [P, H + S], U8)
-        nc.vector.tensor_copy(rows1[:, 0:H].rearrange("p (t m) -> p m t", t=PACK), d_bytes[:].rearrange("p (m t) -> p m t", t=PACK))
         nc.vector.tensor_copy(rows1[:, H : H + S].bitcast(I32), xq_bytes[:].bitcast(I32))
+        nc.vector.tensor_copy(rows1[:, 0:H].rearrange("p (t m) -> p t m", t=PACK), d_bytes[:].rearrange("p (m t) -> p t m", t=PACK))
         place_rows(plane1, rows1, [nc.scalar, nc.sync])
         d_picked = sb("d_picked", [P, H], U32)
         nc.vector.tensor_copy(d_picked[:], d_tab[:].bitcast(U32).indirect(k1_t[:]))
@@ -84,7 +84,7 @@ def tile_picked_pqcduelgmid_none_po_kernel(tc, x_words, x_scales, d_words, d_sca
 
         h_win = []
         for t in range(PACK):
-            acc = psum.tile([P, S], F32, name="h_acc%d" % t)
+            acc = psum.tile([P, S], F32, name="h_acc", tag="h_acc%d" % t)
             cols = slice(P * t, P * t + P)
             nc.tensor.matmul_mx(acc[:], lhsT=d_dealt[:, cols].bitcast(FP8X4), lhsT_scale=plane1[:, cols],
                                 rhs=xq_words[:].bitcast(FP8X4), rhs_scale=plane1[:, H : H + S], start=True, stop=True)
@@ -99,9 +99,10 @@ def tile_picked_pqcduelgmid_none_po_kernel(tc, x_words, x_scales, d_words, d_sca
         ra = [sb("ra%d" % g, [P, 2, W], F32) for g in range(2)]
         rb = [sb("rb%d" % g, [P, 2, W], F32) for g in range(2)]
         dt = [sb("dt%d" % t, [P, S], F32) for t in range(PACK)]
-        z_bf = sb("z_bf", [P, S, PACK], BF16)
-        xc_words = sb("xc_words", [P, C], U32)
-        xc_scales = sb("xc_scales", [P, C], U8)
+        J = S // 2
+        first, second, whole = slice(0, J), slice(J, S), slice(0, S)
+        halves = (first, second)
+        z_bf = [sb("z_bf%d" % hf, [P, J, PACK], BF16) for hf in range(2)]
 
         def fetch(t):
             g, u = divmod(t, 2)
@@ -123,13 +124,8 @@ def tile_picked_pqcduelgmid_none_po_kernel(tc, x_words, x_scales, d_words, d_sca
             nc.scalar.activation(dt[t][:].indirect(lst[:]), src[g][:, u, :], ACT.Copy)
 
         def weigh_round(t):
-            nc.vector.tensor_scalar(z_bf[:, :, t], dt[t][:], gs_t[:, t : t + 1], None, ALU.mult)
-
-        def pick_cand(i):
-            lst = cand_t[:, 16 * i : 16 * i + 16]
-            ms = slice(64 * i, 64 * i + 64)
-            nc.vector.tensor_copy(xc_words[:].rearrange("p (t m) -> p m t", t=PACK)[:, ms, :], x_tab[:].bitcast(U32).indirect(lst))
-            nc.vector.tensor_copy(xc_scales[:].rearrange("p (t m) -> p m t", t=PACK)[:, ms, :], x_scale_tab[:].indirect(lst))
+            for hf, c in enumerate(halves):
+                nc.vector.tensor_scalar(z_bf[hf][:, :, t], dt[t][:, c], gs_t[:, t : t + 1], None, ALU.mult)
 
         fetch(0)
         fetch(1)
@@ -143,9 +139,15 @@ def tile_picked_pqcduelgmid_none_po_kernel(tc, x_words, x_scales, d_words, d_sca
         put(ra, n1_t, 1)
         duel_tanh(1)
         duel_weigh(1)
-        pick_cand(0)
-        pick_cand(1)
-        place_rows(xc_plane, xc_scales, [nc.sync])
+        xc_bytes = sb("xc_bytes", [P, C], U8, tag="pa1")
+        nc.vector.tensor_copy(xc_bytes[:], x_scale_tab[:].indirect(cand_t[:]))
+        xc_rows = sb("xc_rows", [P, C], U8)
+        nc.vector.tensor_copy(xc_rows[:].rearrange("p (t m) -> p t m", t=PACK), xc_bytes[:].rearrange("p (m t) -> p t m", t=PACK))
+        place_rows(xc_plane, xc_rows, [nc.sync])
+        xc_picked = sb("xc_picked", [P, C], U32, tag="npb1")
+        nc.vector.tensor_copy(xc_picked[:], x_tab[:].bitcast(U32).indirect(cand_t[:]))
+        xc_words = sb("xc_words", [P, C], U32)
+        nc.vector.tensor_copy(xc_words[:].rearrange("p (t m) -> p m t", t=PACK), xc_picked[:].rearrange("p (m t) -> p m t", t=PACK))
         put(rb, n2_t, 0)
         put(rb, n2_t, 1)
         weigh_round(0)
@@ -159,17 +161,23 @@ def tile_picked_pqcduelgmid_none_po_kernel(tc, x_words, x_scales, d_words, d_sca
 
         z_words = sb("z_words", [P, S], U32)
         z_scales = sb("z_scales", [P, S], U8)
-        nc.vector.quantize_mx(z_words[:].bitcast(FP8X4), z_scales[:], z_bf[:].rearrange("p j t -> p (j t)"))
+        for hf, c in enumerate(halves):
+            nc.vector.quantize_mx(z_words[:, c].bitcast(FP8X4), z_scales[:, c], z_bf[hf][:].rearrange("p j t -> p (j t)"))
 
-        for t in range(PACK):
-            acc = psum.tile([P, S], F32, name="s_acc%d" % t)
+        def scores(t, c, tag, evac):
+            acc = psum.tile([P, c.stop - c.start], F32, name="s_acc", tag=tag)
             cols = slice(P * t, P * t + P)
             nc.tensor.matmul_mx(acc[:], lhsT=xc_words[:, cols].bitcast(FP8X4), lhsT_scale=xc_plane[:, cols],
-                                rhs=z_words[:].bitcast(FP8X4), rhs_scale=z_scales[:], start=True, stop=True)
-            if t == 0:
-                nc.scalar.activation(s_win[t][:, 0:S], acc[:], ACT.Copy, scale=0.0625)
+                                rhs=z_words[:, c].bitcast(FP8X4), rhs_scale=z_scales[:, c], start=True, stop=True)
+            if evac == "scalar":
+                nc.scalar.activation(s_win[t][:, c], acc[:], ACT.Copy, scale=0.0625)
             else:
-                nc.vector.tensor_scalar(s_win[t][:, 0:S], acc[:], 0.0625, None, ALU.mult)
+                nc.vector.tensor_scalar(s_win[t][:, c], acc[:], 0.0625, None, ALU.mult)
+
+        scores(0, first, "h_acc0", "vector")
+        scores(0, second, "s_acc0", "scalar")
+        for t in range(1, PACK):
+            scores(t, whole, "s_acc%d" % t, "vector")
 
         mb = [sb("mb%d" % t, [P, S, 4], F32) for t in range(PACK)]
         lo2 = [sb("lo2_%d" % t, [P, 2, S], F32) for t in range(PACK)]
@@ -183,8 +191,6 @@ def tile_picked_pqcduelgmid_none_po_kernel(tc, x_words, x_scales, d_words, d_sca
         y_scales = sb("y_scales", [P, S], U8)
         out_rows = out_0.rearrange("(p t) j -> p t j", t=PACK)
         out_words = out_1[0].rearrange("p n t -> p (n t)").bitcast(I32)
-        J = S // 2
-        first, second, whole = slice(0, J), slice(J, S), slice(0, S)
 
         def members(t, c):
             nc.scalar.activation(mb[t][:, c, :].rearrange("p j e -> p (j e)"), s_win[t][:].indirect(n3_t[:, c.start // 4 : c.stop // 4]), ACT.Copy)
@@ -203,37 +209,32 @@ def tile_picked_pqcduelgmid_none_po_kernel(tc, x_words, x_scales, d_words, d_sca
             nc.sync.dma_start(out_rows[:, t, c], y[:, t, c])
 
         def planes(c, cast):
-            cast(y_bf[:, c, :], y[:, :, c].rearrange("p t j -> p j t"))
+            cast(y_bf[:, c, :].rearrange("p (b i) t -> p b t i", i=4), y[:, :, c].rearrange("p t (b i) -> p b t i", i=4))
             nc.vector.quantize_mx(y_words[:, c].bitcast(FP8X4), y_scales[:, c], y_bf[:, c, :].rearrange("p j t -> p (j t)"))
             nc.scalar.dma_start(out_words[:, c], y_words[:, c].bitcast(I32))
 
         last = PACK - 1
+        pending = None
         for t in range(PACK):
-            members(t, first)
-            pair(lo2, t, first, ALU.min)
-            if t:
-                quad(lo, lo2, t - 1, whole, ALU.min)
-            pair(hi2, t, first, ALU.max)
-            if t:
-                quad(hi, hi2, t - 1, whole, ALU.max)
-                larger(t - 1, whole)
-            members(t, second)
-            if t == last:
-                quad(lo, lo2, t, first, ALU.min)
-                result(t - 1, whole)
-                quad(hi, hi2, t, first, ALU.max)
-                larger(t, first)
-            pair(lo2, t, second, ALU.min)
-            if 0 < t < last:
-                result(t - 1, whole)
-            if t == last:
-                result(t, first)
-            pair(hi2, t, second, ALU.max)
-        quad(lo, lo2, last, second, ALU.min)
-        quad(hi, hi2, last, second, ALU.max)
-        larger(last, second)
+            for c in (first, second):
+                members(t, c)
+                if pending:
+                    quad(lo, lo2, *pending, ALU.min)
+                    quad(hi, hi2, *pending, ALU.max)
+                    larger(*pending)
+                pair(lo2, t, c, ALU.min)
+                if pending:
+                    result(*pending)
+                pair(hi2, t, c, ALU.max)
+                if t in (0, last):
+                    pending = (t, c)
+                else:
+                    pending = (t, whole) if c is second else None
+        quad(lo, lo2, *pending, ALU.min)
+        quad(hi, hi2, *pending, ALU.max)
+        larger(*pending)
         planes(first, nc.scalar.copy)
-        result(last, second)
+        result(*pending)
         planes(second, nc.vector.tensor_copy)
         for q in range(4):
             eng = nc.scalar if q % 2 else nc.sync

@@ -77,20 +77,25 @@ def tile_picked_pqcduelgmid_none_po_kernel(tc, x_words, x_scales, d_words, d_sca
         place_rows(plane1, rows1, [nc.scalar, nc.sync])
         d_picked = sb("d_picked", [P, H], U32)
         nc.vector.tensor_copy(d_picked[:], d_tab[:].bitcast(U32).indirect(k1_t[:]))
-        d_dealt = sb("d_dealt", [P, H], U32)
-        nc.vector.tensor_copy(d_dealt[:].rearrange("p (t m) -> p m t", t=PACK), d_picked[:].rearrange("p (m t) -> p m t", t=PACK))
         xq_words = sb("xq_words", [P, S], U32)
         nc.vector.tensor_copy(xq_words[:], x_tab[:].bitcast(U32).indirect(offs_t[:]))
+        d_dealt = [sb("d_dealt%d" % g, [P, 2, P], U32) for g in range(2)]
+        for g in range(2):
+            nc.vector.tensor_copy(d_dealt[g][:].rearrange("p u m -> p m u"), d_picked[:].rearrange("p (m t) -> p m t", t=PACK)[:, :, 2 * g : 2 * g + 2])
 
-        h_win = []
+        J = S // 2
+        first, second, whole = slice(0, J), slice(J, S), slice(0, S)
+        halves = (first, second)
+        h_win = [sb("h_win%d" % t, [P, S], F32) for t in range(PACK)]
+
+        def hidden(t, c, tag):
+            acc = psum.tile([P, c.stop - c.start], F32, name="h_acc", tag=tag)
+            nc.tensor.matmul_mx(acc[:], lhsT=d_dealt[t // 2][:, t % 2, :].bitcast(FP8X4), lhsT_scale=plane1[:, P * t : P * t + P],
+                                rhs=xq_words[:, c].bitcast(FP8X4), rhs_scale=plane1[:, H + c.start : H + c.stop], start=True, stop=True)
+            return acc
+
         for t in range(PACK):
-            acc = psum.tile([P, S], F32, name="h_acc", tag="h_acc%d" % t)
-            cols = slice(P * t, P * t + P)
-            nc.tensor.matmul_mx(acc[:], lhsT=d_dealt[:, cols].bitcast(FP8X4), lhsT_scale=plane1[:, cols],
-                                rhs=xq_words[:].bitcast(FP8X4), rhs_scale=plane1[:, H : H + S], start=True, stop=True)
-            win = sb("h_win%d" % t, [P, S], F32)
-            nc.vector.tensor_scalar(win[:], acc[:], 0.0625 * 0.5, None, ALU.mult)
-            h_win.append(win)
+            nc.vector.tensor_scalar(h_win[t][:], hidden(t, whole, "h_acc%d" % t)[:], 0.0625 * 0.5, None, ALU.mult)
 
         pa = [sb("pa%d" % g, [P, 2, W], F32) for g in range(2)]
         npb = [sb("npb%d" % g, [P, 2, W], F32) for g in range(2)]
@@ -99,9 +104,6 @@ def tile_picked_pqcduelgmid_none_po_kernel(tc, x_words, x_scales, d_words, d_sca
         ra = [sb("ra%d" % g, [P, 2, W], F32) for g in range(2)]
         rb = [sb("rb%d" % g, [P, 2, W], F32) for g in range(2)]
         dt = [sb("dt%d" % t, [P, S], F32) for t in range(PACK)]
-        J = S // 2
-        first, second, whole = slice(0, J), slice(J, S), slice(0, S)
-        halves = (first, second)
         z_bf = [sb("z_bf%d" % hf, [P, J, PACK], BF16) for hf in range(2)]
 
         def fetch(t):
@@ -116,7 +118,8 @@ def tile_picked_pqcduelgmid_none_po_kernel(tc, x_words, x_scales, d_words, d_sca
             nc.scalar.activation(th[g][:], diff[g][:], ACT.Tanh)
 
         def duel_weigh(g):
-            nc.vector.scalar_tensor_tensor(ra[g][:], th[g][:], 1.0, pa[g][:], ALU.add, ALU.mult)
+            for u in range(2) if g == 0 else (slice(0, 2),):
+                nc.vector.scalar_tensor_tensor(ra[g][:, u, :], th[g][:, u, :], 1.0, pa[g][:, u, :], ALU.add, ALU.mult)
             nc.vector.scalar_tensor_tensor(rb[g][:], th[g][:], 1.0, npb[g][:], ALU.subtract, ALU.mult)
 
         def put(src, lst, t):
@@ -164,20 +167,24 @@ def tile_picked_pqcduelgmid_none_po_kernel(tc, x_words, x_scales, d_words, d_sca
         for hf, c in enumerate(halves):
             nc.vector.quantize_mx(z_words[:, c].bitcast(FP8X4), z_scales[:, c], z_bf[hf][:].rearrange("p j t -> p (j t)"))
 
-        def scores(t, c, tag, evac):
+        def scores(t, c, tag):
             acc = psum.tile([P, c.stop - c.start], F32, name="s_acc", tag=tag)
             cols = slice(P * t, P * t + P)
             nc.tensor.matmul_mx(acc[:], lhsT=xc_words[:, cols].bitcast(FP8X4), lhsT_scale=xc_plane[:, cols],
                                 rhs=z_words[:, c].bitcast(FP8X4), rhs_scale=z_scales[:, c], start=True, stop=True)
-            if evac == "scalar":
-                nc.scalar.activation(s_win[t][:, c], acc[:], ACT.Copy, scale=0.0625)
-            else:
-                nc.vector.tensor_scalar(s_win[t][:, c], acc[:], 0.0625, None, ALU.mult)
+            return acc
 
-        scores(0, first, "h_acc0", "vector")
-        scores(0, second, "s_acc0", "scalar")
+        def leave_scalar(t, c, acc):
+            nc.scalar.activation(s_win[t][:, c], acc[:], ACT.Copy, scale=0.0625)
+
+        def leave_vector(t, c, acc):
+            nc.vector.tensor_scalar(s_win[t][:, c], acc[:], 0.0625, None, ALU.mult)
+
+        leave_vector(0, first, scores(0, first, "h_acc0"))
+        leave_scalar(0, second, scores(0, second, "s_acc0"))
+        s_acc = {t: scores(t, whole, "s_acc%d" % t) for t in range(1, PACK)}
         for t in range(1, PACK):
-            scores(t, whole, "s_acc%d" % t, "vector")
+            leave_vector(t, whole, s_acc[t])
 
         mb = [sb("mb%d" % t, [P, S, 4], F32) for t in range(PACK)]
         lo2 = [sb("lo2_%d" % t, [P, 2, S], F32) for t in range(PACK)]
@@ -208,15 +215,18 @@ def tile_picked_pqcduelgmid_none_po_kernel(tc, x_words, x_scales, d_words, d_sca
             nc.vector.scalar_tensor_tensor(y[:, t, c], hi[t][:, c], -0.5, top[t][:, c], ALU.mult, ALU.add)
             nc.sync.dma_start(out_rows[:, t, c], y[:, t, c])
 
-        def planes(c, cast):
+        def regroup(c, cast):
             cast(y_bf[:, c, :].rearrange("p (b i) t -> p b t i", i=4), y[:, :, c].rearrange("p t (b i) -> p b t i", i=4))
+
+        def planes(c):
             nc.vector.quantize_mx(y_words[:, c].bitcast(FP8X4), y_scales[:, c], y_bf[:, c, :].rearrange("p j t -> p (j t)"))
             nc.scalar.dma_start(out_words[:, c], y_words[:, c].bitcast(I32))
 
         last = PACK - 1
+        third, fourth = slice(J, J + J // 2), slice(J + J // 2, S)
         pending = None
         for t in range(PACK):
-            for c in (first, second):
+            for c in (first, third, fourth) if t == last else halves:
                 members(t, c)
                 if pending:
                     quad(lo, lo2, *pending, ALU.min)
@@ -233,9 +243,12 @@ def tile_picked_pqcduelgmid_none_po_kernel(tc, x_words, x_scales, d_words, d_sca
         quad(lo, lo2, *pending, ALU.min)
         quad(hi, hi2, *pending, ALU.max)
         larger(*pending)
-        planes(first, nc.scalar.copy)
+        regroup(first, nc.scalar.copy)
+        regroup(third, nc.scalar.copy)
         result(*pending)
-        planes(second, nc.vector.tensor_copy)
+        planes(first)
+        regroup(fourth, nc.vector.tensor_copy)
+        planes(second)
         for q in range(4):
             eng = nc.scalar if q % 2 else nc.sync
             eng.dma_start(out_2[0, 4 * q : 4 * q + 4, :].bitcast(I32), y_scales[32 * q : 32 * q + 4, :].bitcast(I32))

@@ -34,15 +34,15 @@ def tile_picked_pqcduelgmid_none_po_kernel(tc, x_words, x_scales, d_words, d_sca
             nc.sync.dma_start(t[:], src)
             return t
 
-        offs_t = load_list("offs_t", offs)
         x_scale_tab = sb("x_scale_tab", [P, T], U8)
-        nc.scalar.dma_start(
+        nc.sync.dma_start(
             x_scale_tab[:].bitcast(I32),
             x_scales[0].bitcast(I32).unsqueeze(1).broadcast_to([16, 8, T // 4]),
         )
-        k1_t = load_list("k1_t", k1)
+        offs_t = load_list("offs_t", offs)
         d_scale_tab = sb("d_scale_tab", [P, G], U8)
-        nc.scalar.dma_start(d_scale_tab[:].bitcast(I32), d_scales[0].bitcast(I32).unsqueeze(1).broadcast_to([16, 8, G // 4]))
+        nc.sync.dma_start(d_scale_tab[:].bitcast(I32), d_scales[0].bitcast(I32).unsqueeze(1).broadcast_to([16, 8, G // 4]))
+        k1_t = load_list("k1_t", k1)
         n1_t = load_list("n1_t", n1)
         n2_t = load_list("n2_t", n2)
         d_tab = sb("d_tab", [P, G], I32)
@@ -187,8 +187,8 @@ def tile_picked_pqcduelgmid_none_po_kernel(tc, x_words, x_scales, d_words, d_sca
             leave_vector(t, whole, s_acc[t])
 
         mb = [sb("mb%d" % t, [P, S, 4], F32) for t in range(PACK)]
-        lo2 = [sb("lo2_%d" % t, [P, 2, S], F32) for t in range(PACK)]
-        hi2 = [sb("hi2_%d" % t, [P, 2, S], F32) for t in range(PACK)]
+        lo2 = [sb("lo2_%d" % t, [P, S, 2], F32) for t in range(PACK)]
+        hi2 = [sb("hi2_%d" % t, [P, S, 2], F32) for t in range(PACK)]
         lo = [sb("lo%d" % t, [P, S], F32) for t in range(PACK)]
         hi = [sb("hi%d" % t, [P, S], F32) for t in range(PACK)]
         top = [sb("top%d" % t, [P, S], F32) for t in range(PACK)]
@@ -203,10 +203,10 @@ def tile_picked_pqcduelgmid_none_po_kernel(tc, x_words, x_scales, d_words, d_sca
             nc.scalar.activation(mb[t][:, c, :].rearrange("p j e -> p (j e)"), s_win[t][:].indirect(n3_t[:, c.start // 4 : c.stop // 4]), ACT.Copy)
 
         def pair(dst, t, c, op):
-            nc.vector.tensor_tensor(dst[t][:, :, c].rearrange("p e j -> p j e"), mb[t][:, c, 0:2], mb[t][:, c, 2:4], op)
+            nc.vector.tensor_tensor(dst[t][:, c, :], mb[t][:, c, 0:2], mb[t][:, c, 2:4], op)
 
         def quad(dst, src, t, c, op):
-            nc.vector.tensor_tensor(dst[t][:, c], src[t][:, 0, c], src[t][:, 1, c], op)
+            nc.vector.tensor_tensor(dst[t][:, c], src[t][:, c, 0], src[t][:, c, 1], op)
 
         def larger(t, c):
             nc.vector.tensor_tensor(top[t][:, c], lo[t][:, c], s_win[t][:, c], ALU.max)

from contextlib import ExitStack

import concourse.mybir as mybir

F32 = mybir.dt.float32
BF16 = mybir.dt.bfloat16
I32 = mybir.dt.int32
U32 = mybir.dt.uint32
U16 = mybir.dt.uint16
U8 = mybir.dt.uint8
FP8X4 = mybir.dt.float8_e4m3fn_x4
ALU = mybir.AluOpType
ACT = mybir.ActivationFunctionType

K, T, S, G, H, W, C, U = 512, 1024, 256, 2048, 512, 128, 512, 1024
P = 128
PACK = 4
FLOPS = 2 * K * H * S + 2 * H * C * S
HALF = U // 2
WIN = HALF + 16


def tile_picked_pqcduelgmid_none_po_kernel(tc, x_words, x_scales, d_words, d_scales, gs, offs, k1, n1, n2, cand, n3, out_0, out_1, out_2):
    nc = tc.nc
    with ExitStack() as ctx:
        keep = ctx.enter_context(tc.tile_pool(name="keep", bufs=1))
        psum = ctx.enter_context(tc.psum_pool(name="psum", bufs=1))

        def sb(name, shape, dtype, tag=None):
            return keep.tile(shape, dtype, name=name, tag=tag or name, align_bytes=64)

        def load_list(name, src):
            t = keep.tile(list(src.shape), U16, name=name)
            nc.sync.dma_start(t[:], src)
            return t

        x_scale_tab = sb("x_scale_tab", [P, T], U8)
        nc.sync.dma_start(
            x_scale_tab[:].bitcast(I32),
            x_scales[0].bitcast(I32).unsqueeze(1).broadcast_to([16, 8, T // 4]),
        )
        offs_t = load_list("offs_t", offs)
        d_scale_tab = sb("d_scale_tab", [P, G], U8)
        nc.sync.dma_start(d_scale_tab[:].bitcast(I32), d_scales[0].bitcast(I32).unsqueeze(1).broadcast_to([16, 8, G // 4]))
        k1_t = load_list("k1_t", k1)
        n1_t = load_list("n1_t", n1)
        n2_t = load_list("n2_t", n2)
        d_tab = sb("d_tab", [P, G], I32)
        nc.sync.dma_start(d_tab[:], d_words[0].rearrange("p n t -> p (n t)").bitcast(I32))
        x_tab = sb("x_tab", [P, T], I32)
        nc.sync.dma_start(x_tab[:], x_words[0].rearrange("p n t -> p (n t)").bitcast(I32))
        cand_t = load_list("cand_t", cand)
        n3_t = load_list("n3_t", n3)
        gs_t = sb("gs_t", [P, PACK], F32)
        nc.sync.dma_start(gs_t[:], gs.rearrange("(p t) o -> p (t o)", t=PACK))

        plane1 = sb("plane1", [P, H + S], U8)
        nc.vector.memset(plane1[:].bitcast(I32), 0)
        xc_plane = sb("xc_plane", [P, C], U8)
        nc.vector.memset(xc_plane[:].bitcast(I32), 0)

        def place_rows(plane, rows, engines):
            for a in range(4):
                engines[a % len(engines)].dma_start(plane[a:P:32, :].bitcast(I32), rows[8 * a : P : 32, :].bitcast(I32))

        s_win = [sb("s_win%d" % t, [P, WIN], F32) for t in range(PACK)]
        for t in range(PACK):
            nc.vector.memset(s_win[t][:, S:WIN], 0.0)

        xq_bytes = sb("xq_bytes", [P, S], U8)
        nc.vector.tensor_copy(xq_bytes[:], x_scale_tab[:].indirect(offs_t[:]))
        d_bytes = sb("d_bytes", [P, H], U8)
        nc.vector.tensor_copy(d_bytes[:], d_scale_tab[:].indirect(k1_t[:]))
        rows1 = sb("rows1", [P, H + S], U8)
        nc.vector.tensor_copy(rows1[:, H : H + S].bitcast(I32), xq_bytes[:].bitcast(I32))
        nc.vector.tensor_copy(rows1[:, 0:H].rearrange("p (t m) -> p t m", t=PACK), d_bytes[:].rearrange("p (m t) -> p t m", t=PACK))
        place_rows(plane1, rows1, [nc.scalar, nc.sync])
        d_picked = sb("d_picked", [P, H], U32)
        nc.vector.tensor_copy(d_picked[:], d_tab[:].bitcast(U32).indirect(k1_t[:]))
        xq_words = sb("xq_words", [P, S], U32)
        nc.vector.tensor_copy(xq_words[:], x_tab[:].bitcast(U32).indirect(offs_t[:]))
        d_dealt = [sb("d_dealt%d" % g, [P, 2, P], U32) for g in range(2)]
        for g in range(2):
            nc.vector.tensor_copy(d_dealt[g][:].rearrange("p u m -> p m u"), d_picked[:].rearrange("p (m t) -> p m t", t=PACK)[:, :, 2 * g : 2 * g + 2])

        J = S // 2
        first, second, whole = slice(0, J), slice(J, S), slice(0, S)
        halves = (first, second)
        h_win = [sb("h_win%d" % t, [P, S], F32) for t in range(PACK)]

        def hidden(t, c, tag):
            acc = psum.tile([P, c.stop - c.start], F32, name="h_acc", tag=tag)
            nc.tensor.matmul_mx(acc[:], lhsT=d_dealt[t // 2][:, t % 2, :].bitcast(FP8X4), lhsT_scale=plane1[:, P * t : P * t + P],
                                rhs=xq_words[:, c].bitcast(FP8X4), rhs_scale=plane1[:, H + c.start : H + c.stop], start=True, stop=True)
            return acc

        for t in range(PACK):
            nc.vector.tensor_scalar(h_win[t][:], hidden(t, whole, "h_acc%d" % t)[:], 0.0625 * 0.5, None, ALU.mult)

        pa = [sb("pa%d" % g, [P, 2, W], F32) for g in range(2)]
        npb = [sb("npb%d" % g, [P, 2, W], F32) for g in range(2)]
        diff = [sb("diff%d" % g, [P, 2, W], F32) for g in range(2)]
        th = [sb("th%d" % g, [P, 2, W], F32) for g in range(2)]
        ra = [sb("ra%d" % g, [P, 2, W], F32) for g in range(2)]
        rb = [sb("rb%d" % g, [P, 2, W], F32) for g in range(2)]
        dt = [sb("dt%d" % t, [P, S], F32) for t in range(PACK)]
        z_bf = [sb("z_bf%d" % hf, [P, J, PACK], BF16) for hf in range(2)]

        def fetch(t):
            g, u = divmod(t, 2)
            nc.scalar.activation(pa[g][:, u, :], h_win[t][:].indirect(n1_t[:]), ACT.Copy)
            nc.scalar.activation(npb[g][:, u, :], h_win[t][:].indirect(n2_t[:]), ACT.Copy, scale=-1.0)

        def duel_diff(g):
            nc.vector.tensor_tensor(diff[g][:], pa[g][:], npb[g][:], ALU.add)

        def duel_tanh(g):
            nc.scalar.activation(th[g][:], diff[g][:], ACT.Tanh)

        def duel_weigh(g):
            for u in range(2) if g == 0 else (slice(0, 2),):
                nc.vector.scalar_tensor_tensor(ra[g][:, u, :], th[g][:, u, :], 1.0, pa[g][:, u, :], ALU.add, ALU.mult)
            nc.vector.scalar_tensor_tensor(rb[g][:], th[g][:], 1.0, npb[g][:], ALU.subtract, ALU.mult)

        def put(src, lst, t):
            g, u = divmod(t, 2)
            nc.scalar.activation(dt[t][:].indirect(lst[:]), src[g][:, u, :], ACT.Copy)

        def weigh_round(t):
            for hf, c in enumerate(halves):
                nc.vector.tensor_scalar(z_bf[hf][:, :, t], dt[t][:, c], gs_t[:, t : t + 1], None, ALU.mult)

        fetch(0)
        fetch(1)
        duel_diff(0)
        fetch(2)
        duel_tanh(0)
        duel_weigh(0)
        fetch(3)
        duel_diff(1)
        put(ra, n1_t, 0)
        put(ra, n1_t, 1)
        duel_tanh(1)
        duel_weigh(1)
        xc_bytes = sb("xc_bytes", [P, C], U8, tag="pa1")
        nc.vector.tensor_copy(xc_bytes[:], x_scale_tab[:].indirect(cand_t[:]))
        xc_rows = sb("xc_rows", [P, C], U8)
        nc.vector.tensor_copy(xc_rows[:].rearrange("p (t m) -> p t m", t=PACK), xc_bytes[:].rearrange("p (m t) -> p t m", t=PACK))
        place_rows(xc_plane, xc_rows, [nc.sync])
        xc_picked = sb("xc_picked", [P, C], U32, tag="npb1")
        nc.vector.tensor_copy(xc_picked[:], x_tab[:].bitcast(U32).indirect(cand_t[:]))
        xc_words = sb("xc_words", [P, C], U32)
        nc.vector.tensor_copy(xc_words[:].rearrange("p (t m) -> p m t", t=PACK), xc_picked[:].rearrange("p (m t) -> p m t", t=PACK))
        put(rb, n2_t, 0)
        put(rb, n2_t, 1)
        weigh_round(0)
        weigh_round(1)
        put(ra, n1_t, 2)
        put(ra, n1_t, 3)
        put(rb, n2_t, 2)
        weigh_round(2)
        put(rb, n2_t, 3)
        weigh_round(3)

        z_words = sb("z_words", [P, S], U32)
        z_scales = sb("z_scales", [P, S], U8)
        for hf, c in enumerate(halves):
            nc.vector.quantize_mx(z_words[:, c].bitcast(FP8X4), z_scales[:, c], z_bf[hf][:].rearrange("p j t -> p (j t)"))

        def scores(t, c, tag):
            acc = psum.tile([P, c.stop - c.start], F32, name="s_acc", tag=tag)
            cols = slice(P * t, P * t + P)
            nc.tensor.matmul_mx(acc[:], lhsT=xc_words[:, cols].bitcast(FP8X4), lhsT_scale=xc_plane[:, cols],
                                rhs=z_words[:, c].bitcast(FP8X4), rhs_scale=z_scales[:, c], start=True, stop=True)
            return acc

        def leave_scalar(t, c, acc):
            nc.scalar.activation(s_win[t][:, c], acc[:], ACT.Copy, scale=0.0625)

        def leave_vector(t, c, acc):
            nc.vector.tensor_scalar(s_win[t][:, c], acc[:], 0.0625, None, ALU.mult)

        leave_vector(0, first, scores(0, first, "h_acc0"))
        leave_scalar(0, second, scores(0, second, "s_acc0"))
        s_acc = {t: scores(t, whole, "s_acc%d" % t) for t in range(1, PACK)}
        for t in range(1, PACK):
            leave_vector(t, whole, s_acc[t])

        mb = [sb("mb%d" % t, [P, S, 4], F32) for t in range(PACK)]
        lo2 = [sb("lo2_%d" % t, [P, S, 2], F32) for t in range(PACK)]
        hi2 = [sb("hi2_%d" % t, [P, S, 2], F32) for t in range(PACK)]
        lo = [sb("lo%d" % t, [P, S], F32) for t in range(PACK)]
        hi = [sb("hi%d" % t, [P, S], F32) for t in range(PACK)]
        top = [sb("top%d" % t, [P, S], F32) for t in range(PACK)]
        y = sb("y", [P, PACK, S], F32)
        y_bf = sb("y_bf", [P, S, PACK], BF16)
        y_words = sb("y_words", [P, S], U32)
        y_scales = sb("y_scales", [P, S], U8)
        out_rows = out_0.rearrange("(p t) j -> p t j", t=PACK)
        out_words = out_1[0].rearrange("p n t -> p (n t)").bitcast(I32)

        def members(t, c):
            nc.scalar.activation(mb[t][:, c, :].rearrange("p j e -> p (j e)"), s_win[t][:].indirect(n3_t[:, c.start // 4 : c.stop // 4]), ACT.Copy)

        def pair(dst, t, c, op):
            nc.vector.tensor_tensor(dst[t][:, c, :], mb[t][:, c, 0:2], mb[t][:, c, 2:4], op)

        def quad(dst, src, t, c, op):
            nc.vector.tensor_tensor(dst[t][:, c], src[t][:, c, 0], src[t][:, c, 1], op)

        def larger(t, c):
            nc.vector.tensor_tensor(top[t][:, c], lo[t][:, c], s_win[t][:, c], ALU.max)

        def result(t, c):
            nc.vector.scalar_tensor_tensor(y[:, t, c], hi[t][:, c], -0.5, top[t][:, c], ALU.mult, ALU.add)
            nc.sync.dma_start(out_rows[:, t, c], y[:, t, c])

        def regroup(c, cast):
            cast(y_bf[:, c, :].rearrange("p (b i) t -> p b t i", i=4), y[:, :, c].rearrange("p t (b i) -> p b t i", i=4))

        def planes(c):
            nc.vector.quantize_mx(y_words[:, c].bitcast(FP8X4), y_scales[:, c], y_bf[:, c, :].rearrange("p j t -> p (j t)"))
            nc.scalar.dma_start(out_words[:, c], y_words[:, c].bitcast(I32))

        last = PACK - 1
        third, fourth = slice(J, J + J // 2), slice(J + J // 2, S)
        pending = None
        for t in range(PACK):
            for c in (first, third, fourth) if t == last else halves:
                members(t, c)
                if pending:
                    quad(lo, lo2, *pending, ALU.min)
                    quad(hi, hi2, *pending, ALU.max)
                    larger(*pending)
                pair(lo2, t, c, ALU.min)
                if pending:
                    result(*pending)
                pair(hi2, t, c, ALU.max)
                if t in (0, last):
                    pending = (t, c)
                else:
                    pending = (t, whole) if c is second else None
        quad(lo, lo2, *pending, ALU.min)
        quad(hi, hi2, *pending, ALU.max)
        larger(*pending)
        regroup(first, nc.scalar.copy)
        regroup(third, nc.scalar.copy)
        result(*pending)
        planes(first)
        regroup(fourth, nc.vector.tensor_copy)
        planes(second)
        for q in range(4):
            eng = nc.scalar if q % 2 else nc.sync
            eng.dma_start(out_2[0, 4 * q : 4 * q + 4, :].bitcast(I32), y_scales[32 * q : 32 * q + 4, :].bitcast(I32))
